import numpy as np
import ml_dtypes


def mxq(x, axis, fmt="e4m3"):
    dtype, down = {"e4m3": (ml_dtypes.float8_e4m3fn, 7), "e5m2": (ml_dtypes.float8_e5m2, 14)}[fmt]
    v = np.moveaxis(np.asarray(x, np.float32).astype(ml_dtypes.bfloat16).astype(np.float64), axis, -1)
    blocks = v.reshape(v.shape[:-1] + (-1, 32))
    amax = np.abs(blocks).max(-1, keepdims=True)
    byte = np.maximum(np.where(amax > 0, np.frexp(amax)[1] - 1 + 127, 0) - down, 1)
    scale = np.exp2(byte - 127.0)
    codes = (blocks / scale).astype(np.float32).astype(dtype).astype(np.float64)
    return np.moveaxis((codes * scale).reshape(v.shape), -1, axis)


WIDE = False


def mx_kscale(k):
    if not WIDE:
        return np.ones(k)
    levels = np.array([10, -10, 5, -5, 0])
    if k % 512:
        return np.exp2(np.random.permutation(np.resize(levels, k // 32))).repeat(32)
    a = np.empty((k // 512, 16))
    for p in range(k // 512):
        a[p, :8] = np.random.permutation(np.resize(levels, 8))
        for g in range(8):
            far = levels[np.abs(levels - a[p, g]) >= 10]
            a[p, g + 8] = far[np.random.randint(len(far))]
    return np.exp2(a.ravel()).repeat(32)


def f64(x):
    return np.asarray(x).astype(np.float64)


def striped(idx):
    return np.tile(np.asarray(idx).reshape(-1, 16).T, (8, 1)).astype(np.uint16)


def unstriped(offs):
    return offs[:16].T.reshape(-1).astype(np.int64)


E2M1 = np.array([0.0, 0.5, 1.0, 1.5, 2.0, 3.0, 4.0, 6.0, -0.0, -0.5, -1.0, -1.5, -2.0, -3.0, -4.0, -6.0])


def pack_weight(w, fmt):
    k, n = w.shape
    w = f64(np.asarray(w, np.float32).astype(ml_dtypes.bfloat16)).reshape(k // 32, 32, n)
    amax = np.abs(w).max(1)
    if fmt == "e4m3":
        byte = np.frexp(amax)[1] - 1 + 127 - 7
    else:
        mant, ex = np.frexp(amax / 6.0)
        byte = np.where(mant > 0.5, ex, ex - 1) + 127
    byte = np.clip(np.where(amax > 0, byte, 1), 1, 254)
    scaled = (w * np.exp2(127.0 - byte)[:, None, :]).reshape(k, n).astype(np.float32)
    by_word = np.ascontiguousarray(scaled.reshape(k // 512, 128, 4, n).transpose(0, 1, 3, 2))
    if fmt == "e4m3":
        words = by_word.astype(ml_dtypes.float8_e4m3fn).view(np.uint8)
    else:
        c = by_word.astype(ml_dtypes.float4_e2m1fn).view(np.uint8) & 0xF
        words = (c[..., 0::2] | (c[..., 1::2] << 4)).reshape(k // 512, 128, 2 * n)
    return np.ascontiguousarray(words), np.ascontiguousarray(byte.astype(np.uint8).reshape(k // 512, 16, n))


def unpack_weight(words, scales, fmt):
    g, _, n = scales.shape
    words = np.ascontiguousarray(words).reshape(g, 128, n, -1)
    if fmt == "e4m3":
        vals = words.view(ml_dtypes.float8_e4m3fn).astype(np.float64)
    else:
        nib = np.empty((g, 128, n, 4), np.uint8)
        nib[..., 0::2] = words & 0xF
        nib[..., 1::2] = words >> 4
        vals = E2M1[nib]
    vals = vals * np.repeat(np.exp2(scales.astype(np.float64) - 127.0), 8, axis=1)[..., None]
    return vals.transpose(0, 1, 3, 2).reshape(g * 512, n)


def bf(x):
    return np.asarray(x, np.float32).astype(ml_dtypes.bfloat16)


def planes(Y):
    r, m = Y.shape
    b = f64(bf(Y)).reshape(r // 32, 32, m)
    amax = np.abs(b).max(1)
    byte = np.clip(np.where(amax > 0, np.frexp(amax)[1] - 1 + 127 - 7, 1), 1, 254)
    codes = (b * np.exp2(127.0 - byte)[:, None, :]).reshape(r, m).astype(np.float32).astype(ml_dtypes.float8_e4m3fn).view(np.uint8)
    words = codes.reshape(r // 512, 128, 4, m).transpose(0, 1, 3, 2)
    return np.ascontiguousarray(words), np.ascontiguousarray(byte.astype(np.uint8).reshape(r // 512, 16, m))


K, R, F, T, J, G = 512, 512, 512, 2048, 256, 16


def setup_inputs():
    n = np.random.standard_normal
    idx = np.random.permutation(T)[:J]
    fk = mx_kscale(K)
    fr = mx_kscale(R)
    dtabp = pack_weight(n((K, T)) / fk[:, None], "e4m3")
    tabp = pack_weight(n((K, T)) / fk[:, None], "e4m3")
    return {
        "dtab_words": dtabp[0],
        "dtab_scales": dtabp[1],
        "tab_words": tabp[0],
        "tab_scales": tabp[1],
        "w1": (n((K, R)) * 1 / np.sqrt(K) * fk[:, None]).astype(np.float32),
        "sharp": (np.random.uniform(0.3, 1.5, (R, 1))).astype(np.float32),
        "rs": (np.random.uniform(0.5, 2.0, (R, 1)) * fr[:, None]).astype(np.float32),
        "wor": (n((R, F)) * 1 / np.sqrt(R) / fr[:, None]).astype(np.float32),
        "res": (n((F, J)) * 0.5).astype(np.float32),
        "offs": striped(idx),
    }


def reference(dtab_words, dtab_scales, tab_words, tab_scales, w1, sharp, rs, wor, res, offs):
    idx = unstriped(offs)
    dtabu = unpack_weight(dtab_words, dtab_scales, "e4m3")
    tabu = unpack_weight(tab_words, tab_scales, "e4m3")
    w1q = mxq(f64(w1), 0, "e4m3")
    tabidxg = tabu[:, idx]
    a = w1q.T @ tabidxg
    dtabidxg = dtabu[:, idx]
    ta = w1q.T @ dtabidxg
    m1 = a.reshape(R, G, J // G).mean(axis=2)
    mr = np.repeat(m1, J // G, axis=1)
    ce = a - mr
    tm1 = ta.reshape(R, G, J // G).mean(axis=2)
    tmr = np.repeat(tm1, J // G, axis=1)
    tce = ta - tmr
    tu1 = (ta - tce * ce * 2.0 * f64(sharp) * a / (np.square(ce) * f64(sharp) + 1.0)) / (np.square(ce) * f64(sharp) + 1.0)
    fo1 = tu1 * f64(rs)
    worq = mxq(f64(wor), 0, "e4m3")
    fo1q = mxq(fo1, 0, "e4m3")
    yo = worq.T @ fo1q
    y = yo + f64(res)
    words, scales = planes(y)
    return y, words, scales

@@ -1,0 +1,215 @@
+from contextlib import ExitStack
+
+import concourse.mybir as mybir
+
+F32 = mybir.dt.float32
+BF16 = mybir.dt.bfloat16
+I32 = mybir.dt.int32
+U32 = mybir.dt.uint32
+U16 = mybir.dt.uint16
+U8 = mybir.dt.uint8
+FP8X4 = mybir.dt.float8_e4m3fn_x4
+ALU = mybir.AluOpType
+ACT = mybir.ActivationFunctionType
+AXX = mybir.AxisListType.X
+
+P = 128
+K, R, F, T, J, G = 512, 512, 512, 2048, 256, 16
+GS = J // G
+H = J // 2
+FLOPS = 2 * (2 * K * R * J + R * F * J)
+M_SPLIT = 80
+PIECES = ((0, 128), (128, 64), (192, 64))
+
+
+def tile_attend_tcontrastpool_o_pl_kernel(tc, dtab_words, dtab_scales, tab_words, tab_scales, w1, sharp, rs, wor, res, offs,
+                                           out_0, out_1, out_2):
+    nc = tc.nc
+    with ExitStack() as ctx:
+        held = ctx.enter_context(tc.tile_pool(name="held", bufs=1))
+        sb = ctx.enter_context(tc.tile_pool(name="sb", bufs=1))
+        ps = ctx.enter_context(tc.psum_pool(name="ps", bufs=1))
+
+        offsets = held.tile([P, J // 16], U16, name="offsets")
+        nc.sync.dma_start(offsets[:], offs)
+
+        ts = sb.tile([P, T], U8, name="ts", align_bytes=64)
+        ds = sb.tile([P, T], U8, name="ds", align_bytes=64)
+        nc.vector.memset(ts[:].bitcast(I32), 0)
+        warm = sb.tile([P, 1], F32, name="warm")
+        warm2 = sb.tile([P, 1], F32, name="warm2")
+        nc.vector.memset(warm[:], 1.0)
+        nc.vector.memset(ds[:].bitcast(I32), 0)
+        for q in range(4):
+            nc.scalar.dma_start(ts[32 * q:32 * q + 4, :].bitcast(I32), tab_scales[0, 4 * q:4 * q + 4, :].bitcast(I32))
+        nc.scalar.activation(warm2[:], warm[:], ACT.Abs_reciprocal_sqrt)
+
+        w1r = sb.tile([P, 4, R], F32, name="w1r", tag="wraw")
+        nc.sync.dma_start(w1r[:], w1.rearrange("(p j) c -> p j c", j=4))
+        tw = sb.tile([P, T], U32, name="tw", tag="tabres", align_bytes=64)
+        nc.sync.dma_start(tw[:].bitcast(I32), tab_words[0].rearrange("p n t -> p (n t)").bitcast(I32))
+        for q in range(4):
+            nc.gpsimd.dma_start(ds[32 * q + 4:32 * q + 8, :].bitcast(I32), dtab_scales[0, 4 * q:4 * q + 4, :].bitcast(I32))
+        dw = sb.tile([P, T], U32, name="dw", align_bytes=64)
+        nc.sync.dma_start(dw[:].bitcast(I32), dtab_words[0].rearrange("p n t -> p (n t)").bitcast(I32))
+        sh = sb.tile([P, 4], F32, name="sh")
+        rr = sb.tile([P, 4], F32, name="rr")
+        nc.gpsimd.dma_start(sh[:], sharp.rearrange("(p t) o -> p (t o)", t=4))
+        nc.gpsimd.dma_start(rr[:], rs.rearrange("(p t) o -> p (t o)", t=4))
+
+        gts = sb.tile([P, J], U8, name="gts", align_bytes=64)
+        gds = sb.tile([P, J], U8, name="gds", align_bytes=64)
+        gtw = sb.tile([P, J], U32, name="gtw", align_bytes=64)
+        gdw = sb.tile([P, J], U32, name="gdw", align_bytes=64)
+        nc.vector.tensor_copy(gts[:], ts[:].indirect(offsets[:]))
+
+        w1g = sb.tile([P, 4, P, 4], BF16, name="w1g", align_bytes=64)
+        w1o = w1g[:].rearrange("p t m j -> p m j t")
+        w1i = w1r[:].rearrange("p j (m t) -> p m j t", t=4)
+        nc.vector.tensor_copy(w1o[:, :M_SPLIT], w1i[:, :M_SPLIT])
+        nc.scalar.copy(w1o[:, M_SPLIT:], w1i[:, M_SPLIT:])
+        wor_r = sb.tile([P, 4, F], F32, name="wor_r", tag="wraw")
+        nc.sync.dma_start(wor_r[:], wor.rearrange("(p j) c -> p j c", j=4))
+        nc.vector.tensor_copy(gds[:], ds[:].indirect(offsets[:]))
+        w1c = sb.tile([P, R], U32, name="w1c", align_bytes=64)
+        w1s = sb.tile([P, R], U8, name="w1s", align_bytes=64)
+        nc.vector.quantize_mx(w1c[:].bitcast(FP8X4), w1s[:], w1g[:].rearrange("p t m j -> p (t m j)"))
+        nc.vector.tensor_copy(gtw[:], tw[:].indirect(offsets[:]))
+        rest = sb.tile([P, 4, J], F32, name="rest", tag="tabres", align_bytes=64)
+        nc.sync.dma_start(rest[:], res.rearrange("(p t) j -> p t j", t=4))
+
+        srs = sb.tile([P, 4], F32, name="srs")
+        s2 = sb.tile([P, 4], F32, name="s2")
+        nc.gpsimd.tensor_tensor(srs[:], sh[:], rr[:], ALU.mult)
+        nc.gpsimd.tensor_scalar(s2[:], srs[:], -2.0, 0.0, ALU.mult, ALU.add)
+
+        A = [ps.tile([P, 2, J], F32, name="A%d" % b) for b in range(2)]
+        for t in range(4):
+            nc.tensor.matmul_mx(A[t // 2][:, t % 2, :], lhsT=w1c[:, t * P:(t + 1) * P].bitcast(FP8X4), lhsT_scale=w1s[:, t * P:(t + 1) * P],
+                                rhs=gtw[:].bitcast(FP8X4), rhs_scale=gts[:], start=True, stop=True)
+
+        S = [sb.tile([P, 2 * G], F32, name="S%d" % b) for b in range(2)]
+        ce = [sb.tile([P, 2, J], F32, name="ce%d" % b) for b in range(2)]
+        sq = [sb.tile([P, 2, J], F32, name="sq%d" % b) for b in range(2)]
+        c1 = sb.tile([P, 4, J], F32, name="c1")
+        dp = sb.tile([P, 4, J], F32, name="dp")
+        dd = sb.tile([P, 4, J], F32, name="dd")
+        yy = sb.tile([P, 4, J], F32, name="yy")
+        qq = sb.tile([P, 4, J], F32, name="qq")
+        uu = sb.tile([P, 4, J], F32, name="uu")
+        for b in range(2):
+            nc.vector.tensor_reduce(S[b][:], A[b][:].rearrange("p t (g i) -> p (t g) i", i=GS), AXX, ALU.add)
+        for b in range(2):
+            nc.vector.scalar_tensor_tensor(ce[b][:].rearrange("p t (g i) -> p (t g) i", i=GS),
+                                           S[b][:].unsqueeze(2).to_broadcast([P, 2 * G, GS]), -1.0 / GS,
+                                           A[b][:].rearrange("p t (g i) -> p (t g) i", i=GS), ALU.mult, ALU.add)
+            nc.scalar.activation(sq[b][:], ce[b][:], ACT.Square)
+            for t in (2 * b, 2 * b + 1):
+                nc.scalar.activation(dp[:, t, :], sq[b][:, t % 2, :], ACT.Identity, bias=rr[:, t:t + 1], scale=srs[:, t:t + 1])
+        nc.vector.tensor_copy(gdw[:], dw[:].indirect(offsets[:]))
+        TA = [ps.tile([P, 4, H], F32, name="TA%d" % h) for h in range(2)]
+        for h in range(2):
+            for t in range(4):
+                nc.tensor.matmul_mx(TA[h][:, t, :], lhsT=w1c[:, t * P:(t + 1) * P].bitcast(FP8X4), lhsT_scale=w1s[:, t * P:(t + 1) * P],
+                                    rhs=gdw[:, h * H:(h + 1) * H].bitcast(FP8X4), rhs_scale=gds[4:P, h * H:(h + 1) * H], start=True, stop=True)
+        for t in range(4):
+            nc.vector.scalar_tensor_tensor(c1[:, t, :], ce[t // 2][:, t % 2, :], s2[:, t:t + 1], A[t // 2][:, t % 2, :], ALU.mult, ALU.mult)
+        for t in range(4):
+            nc.scalar.activation(dd[:, t, :], sq[t // 2][:, t % 2, :], ACT.Square, bias=1.0, scale=sh[:, t:t + 1])
+        for h in range(2):
+            js = slice(h * H, (h + 1) * H)
+            nc.scalar.activation(yy[:, :, js], dd[:, :, js], ACT.Abs_reciprocal_sqrt)
+            nc.scalar.activation(qq[:, :, js], yy[:, :, js], ACT.Square)
+
+        worg = sb.tile([P, 4, P, 4], BF16, name="worg", align_bytes=64)
+        woro = worg[:].rearrange("p t m j -> p m j t")
+        wori = wor_r[:].rearrange("p j (m t) -> p m j t", t=4)
+        for c in range(2):
+            nc.scalar.copy(woro[:, c * 64:(c + 1) * 64], wori[:, c * 64:(c + 1) * 64])
+
+        TS = [sb.tile([P, 4, G // 2], F32, name="TS%d" % h) for h in range(2)]
+        NP = len(PIECES)
+        x1 = [sb.tile([P, 4, w], F32, name="x1%d" % n) for n, (j0, w) in enumerate(PIECES)]
+        x2 = [sb.tile([P, 4, w], F32, name="x2%d" % n) for n, (j0, w) in enumerate(PIECES)]
+        x3 = [sb.tile([P, 4, w], F32, name="x3%d" % n) for n, (j0, w) in enumerate(PIECES)]
+        fo = [sb.tile([P, w, 4], BF16, name="fo%d" % n, align_bytes=64) for n, (j0, w) in enumerate(PIECES)]
+        foc = [sb.tile([P, w], U32, name="foc%d" % n, align_bytes=64) for n, (j0, w) in enumerate(PIECES)]
+        fos = [sb.tile([P, w], U8, name="fos%d" % n, align_bytes=64) for n, (j0, w) in enumerate(PIECES)]
+        Y = [ps.tile([P, 4, w], F32, name="Y%d" % n) for n, (j0, w) in enumerate(PIECES)]
+        y = [sb.tile([P, 4, w], F32, name="y%d" % n) for n, (j0, w) in enumerate(PIECES)]
+        yb = [sb.tile([P, w, 4], BF16, name="yb%d" % n, align_bytes=64) for n, (j0, w) in enumerate(PIECES)]
+        for h in range(2):
+            nc.vector.tensor_reduce(TS[h][:].rearrange("p t g -> p (t g)"), TA[h][:].rearrange("p t (g i) -> p (t g) i", i=GS), AXX, ALU.add)
+        nc.vector.tensor_tensor(uu[:], dp[:], c1[:], ALU.add)
+        worc = sb.tile([P, F], U32, name="worc", align_bytes=64)
+        wors = sb.tile([P, F], U8, name="wors", align_bytes=64)
+        yc = sb.tile([P, J], U32, name="yc", align_bytes=64)
+        ys = sb.tile([P, J], U8, name="ys", align_bytes=64)
+        o0 = out_0.rearrange("(p t) j -> p t j", t=4)
+        o1 = out_1[0].rearrange("p n t -> p (n t)").bitcast(I32)
+
+        def il(ap):
+            return ap.rearrange("p t (c i) -> p c t i", i=4)
+
+        def ilo(ap):
+            return ap.rearrange("p (c i) t -> p c t i", i=4)
+
+        def products(n):
+            j0, w = PIECES[n]
+            h, b0 = divmod(j0, H)
+            nc.vector.tensor_tensor(x2[n][:].rearrange("p t (g i) -> p t g i", i=GS),
+                                    c1[:, :, j0:j0 + w].rearrange("p t (g i) -> p t g i", i=GS),
+                                    TS[h][:, :, b0 // GS:(b0 + w) // GS].unsqueeze(3).to_broadcast([P, 4, w // GS, GS]), ALU.mult)
+            nc.vector.tensor_tensor(x1[n][:], TA[h][:, :, b0:b0 + w], uu[:, :, j0:j0 + w], ALU.mult)
+
+        def combine(n):
+            nc.vector.scalar_tensor_tensor(x3[n][:].rearrange("p t j -> p (t j)"), x2[n][:].rearrange("p t j -> p (t j)"), -1.0 / GS,
+                                           x1[n][:].rearrange("p t j -> p (t j)"), ALU.mult, ALU.add)
+
+        def scale(n):
+            j0, w = PIECES[n]
+            nc.vector.tensor_tensor(ilo(fo[n][:]), il(x3[n][:]), il(qq[:, :, j0:j0 + w]), ALU.mult)
+
+        def layer2(n):
+            nc.vector.quantize_mx(foc[n][:].bitcast(FP8X4), fos[n][:], fo[n][:].rearrange("p j t -> p (j t)"))
+            for t in range(4):
+                nc.tensor.matmul_mx(Y[n][:, t, :], lhsT=worc[:, t * P:(t + 1) * P].bitcast(FP8X4), lhsT_scale=wors[:, t * P:(t + 1) * P],
+                                    rhs=foc[n][:].bitcast(FP8X4), rhs_scale=fos[n][:], start=True, stop=True)
+
+        def residual(n):
+            j0, w = PIECES[n]
+            if n == NP - 1:
+                nc.vector.tensor_tensor(ilo(yb[n][:]), il(Y[n][:]), il(rest[:, :, j0:j0 + w]), ALU.add)
+            nc.vector.tensor_tensor(y[n][:], Y[n][:], rest[:, :, j0:j0 + w], ALU.add)
+            nc.sync.dma_start(o0[:, :, j0:j0 + w], y[n][:])
+            if n < NP - 1:
+                nc.scalar.copy(ilo(yb[n][:]), il(y[n][:]))
+
+        def planes(n):
+            j0, w = PIECES[n]
+            nc.vector.quantize_mx(yc[:, j0:j0 + w].bitcast(FP8X4), ys[:, j0:j0 + w], yb[n][:].rearrange("p j t -> p (j t)"))
+
+        products(0)
+        products(1)
+        combine(0)
+        combine(1)
+        scale(0)
+        nc.vector.quantize_mx(worc[:].bitcast(FP8X4), wors[:], worg[:].rearrange("p t m j -> p (t m j)"))
+        layer2(0)
+        scale(1)
+        products(2)
+        layer2(1)
+        combine(2)
+        residual(0)
+        scale(2)
+        residual(1)
+        layer2(2)
+        planes(0)
+        planes(1)
+        nc.scalar.dma_start(o1[:, 0:192], yc[:, 0:192].bitcast(I32))
+        residual(2)
+        planes(2)
+        nc.sync.dma_start(o1[:, 192:J], yc[:, 192:J].bitcast(I32))
+        for q in range(4):
+            eng = nc.sync if q == 3 else nc.scalar
+            eng.dma_start(out_2[0, 4 * q:4 * q + 4, :].bitcast(I32), ys[32 * q:32 * q + 4, :].bitcast(I32))

@@ -34,48 +34,48 @@ def tile_attend_tcontrastpool_o_pl_kernel(tc, dtab_words, dtab_scales, tab_words
         nc.sync.dma_start(offsets[:], offs)
 
         ts = sb.tile([P, T], U8, name="ts", align_bytes=64)
-        ds = sb.tile([P, T], U8, name="ds", align_bytes=64)
         nc.vector.memset(ts[:].bitcast(I32), 0)
-        warm = sb.tile([P, 1], F32, name="warm")
-        warm2 = sb.tile([P, 1], F32, name="warm2")
+        warm = sb.tile([P, 1], F32, name="warm", tag="tabres", align_bytes=64)
+        warm2 = sb.tile([P, 1], F32, name="warm2", tag="dsres", align_bytes=64)
         nc.vector.memset(warm[:], 1.0)
-        nc.vector.memset(ds[:].bitcast(I32), 0)
-        for q in range(4):
-            nc.scalar.dma_start(ts[32 * q:32 * q + 4, :].bitcast(I32), tab_scales[0, 4 * q:4 * q + 4, :].bitcast(I32))
         nc.scalar.activation(warm2[:], warm[:], ACT.Abs_reciprocal_sqrt)
 
-        w1r = sb.tile([P, 4, R], F32, name="w1r", tag="wraw")
+        w1r = sb.tile([P, 4, R], F32, name="w1r", tag="wraw", align_bytes=64)
         nc.sync.dma_start(w1r[:], w1.rearrange("(p j) c -> p j c", j=4))
+        for q in range(4):
+            nc.sync.dma_start(ts[q:P:32, :].bitcast(I32), tab_scales[0, q:16:4, :].bitcast(I32))
         tw = sb.tile([P, T], U32, name="tw", tag="tabres", align_bytes=64)
         nc.sync.dma_start(tw[:].bitcast(I32), tab_words[0].rearrange("p n t -> p (n t)").bitcast(I32))
+        ds = sb.tile([P, T], U8, name="ds", tag="dsres", align_bytes=64)
+        nc.vector.memset(ds[:].bitcast(I32), 0)
         for q in range(4):
-            nc.gpsimd.dma_start(ds[32 * q + 4:32 * q + 8, :].bitcast(I32), dtab_scales[0, 4 * q:4 * q + 4, :].bitcast(I32))
-        dw = sb.tile([P, T], U32, name="dw", align_bytes=64)
-        nc.sync.dma_start(dw[:].bitcast(I32), dtab_words[0].rearrange("p n t -> p (n t)").bitcast(I32))
+            nc.scalar.dma_start(ds[4 + q:P:32, :].bitcast(I32), dtab_scales[0, q:16:4, :].bitcast(I32))
         sh = sb.tile([P, 4], F32, name="sh")
         rr = sb.tile([P, 4], F32, name="rr")
         nc.gpsimd.dma_start(sh[:], sharp.rearrange("(p t) o -> p (t o)", t=4))
         nc.gpsimd.dma_start(rr[:], rs.rearrange("(p t) o -> p (t o)", t=4))
 
         gts = sb.tile([P, J], U8, name="gts", align_bytes=64)
-        gds = sb.tile([P, J], U8, name="gds", align_bytes=64)
         gtw = sb.tile([P, J], U32, name="gtw", align_bytes=64)
         gdw = sb.tile([P, J], U32, name="gdw", align_bytes=64)
         nc.vector.tensor_copy(gts[:], ts[:].indirect(offsets[:]))
 
-        w1g = sb.tile([P, 4, P, 4], BF16, name="w1g", align_bytes=64)
+        w1g = sb.tile([P, 4, P, 4], BF16, name="w1g", tag="w1g", align_bytes=64)
         w1o = w1g[:].rearrange("p t m j -> p m j t")
         w1i = w1r[:].rearrange("p j (m t) -> p m j t", t=4)
         nc.vector.tensor_copy(w1o[:, :M_SPLIT], w1i[:, :M_SPLIT])
         nc.scalar.copy(w1o[:, M_SPLIT:], w1i[:, M_SPLIT:])
-        wor_r = sb.tile([P, 4, F], F32, name="wor_r", tag="wraw")
-        nc.sync.dma_start(wor_r[:], wor.rearrange("(p j) c -> p j c", j=4))
-        nc.vector.tensor_copy(gds[:], ds[:].indirect(offsets[:]))
+        dw = sb.tile([P, T], U32, name="dw", tag="wraw", align_bytes=64)
+        nc.sync.dma_start(dw[:].bitcast(I32), dtab_words[0].rearrange("p n t -> p (n t)").bitcast(I32))
         w1c = sb.tile([P, R], U32, name="w1c", align_bytes=64)
         w1s = sb.tile([P, R], U8, name="w1s", align_bytes=64)
         nc.vector.quantize_mx(w1c[:].bitcast(FP8X4), w1s[:], w1g[:].rearrange("p t m j -> p (t m j)"))
+        wor_r = sb.tile([P, 4, F], F32, name="wor_r", tag="w1g", align_bytes=64)
+        nc.sync.dma_start(wor_r[:], wor.rearrange("(p j) c -> p j c", j=4))
         nc.vector.tensor_copy(gtw[:], tw[:].indirect(offsets[:]))
-        rest = sb.tile([P, 4, J], F32, name="rest", tag="tabres", align_bytes=64)
+        gds = sb.tile([P, J], U8, name="gds", tag="tabres", align_bytes=64)
+        nc.vector.tensor_copy(gds[:], ds[:].indirect(offsets[:]))
+        rest = sb.tile([P, 4, J], F32, name="rest", tag="dsres", align_bytes=64)
         nc.sync.dma_start(rest[:], res.rearrange("(p t) j -> p t j", t=4))
 
         srs = sb.tile([P, 4], F32, name="srs")
@@ -105,7 +105,8 @@ def tile_attend_tcontrastpool_o_pl_kernel(tc, dtab_words, dtab_scales, tab_words
                                            A[b][:].rearrange("p t (g i) -> p (t g) i", i=GS), ALU.mult, ALU.add)
             nc.scalar.activation(sq[b][:], ce[b][:], ACT.Square)
             for t in (2 * b, 2 * b + 1):
-                nc.scalar.activation(dp[:, t, :], sq[b][:, t % 2, :], ACT.Identity, bias=rr[:, t:t + 1], scale=srs[:, t:t + 1])
+                nc.gpsimd.tensor_scalar(dp[:, t, :], sq[b][:, t % 2, :], srs[:, t:t + 1], rr[:, t:t + 1], ALU.mult, ALU.add)
+                nc.scalar.activation(dd[:, t, :], sq[t // 2][:, t % 2, :], ACT.Square, bias=1.0, scale=sh[:, t:t + 1])
         nc.vector.tensor_copy(gdw[:], dw[:].indirect(offsets[:]))
         TA = [ps.tile([P, 4, H], F32, name="TA%d" % h) for h in range(2)]
         for h in range(2):
@@ -114,18 +115,15 @@ def tile_attend_tcontrastpool_o_pl_kernel(tc, dtab_words, dtab_scales, tab_words
                                     rhs=gdw[:, h * H:(h + 1) * H].bitcast(FP8X4), rhs_scale=gds[4:P, h * H:(h + 1) * H], start=True, stop=True)
         for t in range(4):
             nc.vector.scalar_tensor_tensor(c1[:, t, :], ce[t // 2][:, t % 2, :], s2[:, t:t + 1], A[t // 2][:, t % 2, :], ALU.mult, ALU.mult)
-        for t in range(4):
-            nc.scalar.activation(dd[:, t, :], sq[t // 2][:, t % 2, :], ACT.Square, bias=1.0, scale=sh[:, t:t + 1])
+        worg = sb.tile([P, 4, P, 4], BF16, name="worg", align_bytes=64)
+        woro = worg[:].rearrange("p t m j -> p m j t")
+        wori = wor_r[:].rearrange("p j (m t) -> p m j t", t=4)
         for h in range(2):
             js = slice(h * H, (h + 1) * H)
             nc.scalar.activation(yy[:, :, js], dd[:, :, js], ACT.Abs_reciprocal_sqrt)
             nc.scalar.activation(qq[:, :, js], yy[:, :, js], ACT.Square)
-
-        worg = sb.tile([P, 4, P, 4], BF16, name="worg", align_bytes=64)
-        woro = worg[:].rearrange("p t m j -> p m j t")
-        wori = wor_r[:].rearrange("p j (m t) -> p m j t", t=4)
-        for c in range(2):
-            nc.scalar.copy(woro[:, c * 64:(c + 1) * 64], wori[:, c * 64:(c + 1) * 64])
+            if h == 0:
+                nc.scalar.copy(woro, wori)
 
         TS = [sb.tile([P, 4, G // 2], F32, name="TS%d" % h) for h in range(2)]
         NP = len(PIECES)

@@ -19,6 +19,7 @@ GS = J // G
 H = J // 2
 FLOPS = 2 * (2 * K * R * J + R * F * J)
 M_SPLIT = 80
+SLOTS = ((0, 1), (1, 1), (2, 2))
 PIECES = ((0, 128), (128, 64), (192, 64))
 
 
@@ -35,21 +36,27 @@ def tile_attend_tcontrastpool_o_pl_kernel(tc, dtab_words, dtab_scales, tab_words
 
         ts = sb.tile([P, T], U8, name="ts", align_bytes=64)
         nc.vector.memset(ts[:].bitcast(I32), 0)
-        warm = sb.tile([P, 1], F32, name="warm", tag="tabres", align_bytes=64)
-        warm2 = sb.tile([P, 1], F32, name="warm2", tag="dsres", align_bytes=64)
+        warm = sb.tile([P, 1], F32, name="warm")
+        warm2 = sb.tile([P, 1], F32, name="warm2")
         nc.vector.memset(warm[:], 1.0)
         nc.scalar.activation(warm2[:], warm[:], ACT.Abs_reciprocal_sqrt)
 
-        w1r = sb.tile([P, 4, R], F32, name="w1r", tag="wraw", align_bytes=64)
+        w1r = sb.tile([P, 4, R], F32, name="w1r")
         nc.sync.dma_start(w1r[:], w1.rearrange("(p j) c -> p j c", j=4))
         for q in range(4):
             nc.sync.dma_start(ts[q:P:32, :].bitcast(I32), tab_scales[0, q:16:4, :].bitcast(I32))
-        tw = sb.tile([P, T], U32, name="tw", tag="tabres", align_bytes=64)
+        tw = sb.tile([P, T], U32, name="tw", align_bytes=64)
         nc.sync.dma_start(tw[:].bitcast(I32), tab_words[0].rearrange("p n t -> p (n t)").bitcast(I32))
         ds = sb.tile([P, T], U8, name="ds", tag="dsres", align_bytes=64)
         nc.vector.memset(ds[:].bitcast(I32), 0)
         for q in range(4):
-            nc.scalar.dma_start(ds[4 + q:P:32, :].bitcast(I32), dtab_scales[0, q:16:4, :].bitcast(I32))
+            nc.sync.dma_start(ds[4 + q:P:32, :].bitcast(I32), dtab_scales[0, q:16:4, :].bitcast(I32))
+        dw = sb.tile([P, T], U32, name="dw", align_bytes=64)
+        nc.sync.dma_start(dw[:].bitcast(I32), dtab_words[0].rearrange("p n t -> p (n t)").bitcast(I32))
+        wor_r = sb.tile([P, 4, F], F32, name="wor_r")
+        nc.sync.dma_start(wor_r[:], wor.rearrange("(p j) c -> p j c", j=4))
+        rest = sb.tile([P, 4, J], F32, name="rest")
+        nc.sync.dma_start(rest[:], res.rearrange("(p t) j -> p t j", t=4))
         sh = sb.tile([P, 4], F32, name="sh")
         rr = sb.tile([P, 4], F32, name="rr")
         nc.gpsimd.dma_start(sh[:], sharp.rearrange("(p t) o -> p (t o)", t=4))
@@ -60,53 +67,67 @@ def tile_attend_tcontrastpool_o_pl_kernel(tc, dtab_words, dtab_scales, tab_words
         gdw = sb.tile([P, J], U32, name="gdw", align_bytes=64)
         nc.vector.tensor_copy(gts[:], ts[:].indirect(offsets[:]))
 
-        w1g = sb.tile([P, 4, P, 4], BF16, name="w1g", tag="w1g", align_bytes=64)
+        w1g = sb.tile([P, 4, P, 4], BF16, name="w1g", align_bytes=64)
         w1o = w1g[:].rearrange("p t m j -> p m j t")
         w1i = w1r[:].rearrange("p j (m t) -> p m j t", t=4)
         nc.vector.tensor_copy(w1o[:, :M_SPLIT], w1i[:, :M_SPLIT])
         nc.scalar.copy(w1o[:, M_SPLIT:], w1i[:, M_SPLIT:])
-        dw = sb.tile([P, T], U32, name="dw", tag="wraw", align_bytes=64)
-        nc.sync.dma_start(dw[:].bitcast(I32), dtab_words[0].rearrange("p n t -> p (n t)").bitcast(I32))
         w1c = sb.tile([P, R], U32, name="w1c", align_bytes=64)
         w1s = sb.tile([P, R], U8, name="w1s", align_bytes=64)
         nc.vector.quantize_mx(w1c[:].bitcast(FP8X4), w1s[:], w1g[:].rearrange("p t m j -> p (t m j)"))
-        wor_r = sb.tile([P, 4, F], F32, name="wor_r", tag="w1g", align_bytes=64)
-        nc.sync.dma_start(wor_r[:], wor.rearrange("(p j) c -> p j c", j=4))
         nc.vector.tensor_copy(gtw[:], tw[:].indirect(offsets[:]))
-        gds = sb.tile([P, J], U8, name="gds", tag="tabres", align_bytes=64)
+        gds = sb.tile([P, J], U8, name="gds", align_bytes=64)
         nc.vector.tensor_copy(gds[:], ds[:].indirect(offsets[:]))
-        rest = sb.tile([P, 4, J], F32, name="rest", tag="dsres", align_bytes=64)
-        nc.sync.dma_start(rest[:], res.rearrange("(p t) j -> p t j", t=4))
 
         srs = sb.tile([P, 4], F32, name="srs")
         s2 = sb.tile([P, 4], F32, name="s2")
         nc.gpsimd.tensor_tensor(srs[:], sh[:], rr[:], ALU.mult)
         nc.gpsimd.tensor_scalar(s2[:], srs[:], -2.0, 0.0, ALU.mult, ALU.add)
 
-        A = [ps.tile([P, 2, J], F32, name="A%d" % b) for b in range(2)]
+        A = [ps.tile([P, n, J], F32, name="A%d" % t0) for t0, n in SLOTS]
+        At = [A[b][:, i, :] for b, (t0, n) in enumerate(SLOTS) for i in range(n)]
         for t in range(4):
-            nc.tensor.matmul_mx(A[t // 2][:, t % 2, :], lhsT=w1c[:, t * P:(t + 1) * P].bitcast(FP8X4), lhsT_scale=w1s[:, t * P:(t + 1) * P],
+            nc.tensor.matmul_mx(At[t], lhsT=w1c[:, t * P:(t + 1) * P].bitcast(FP8X4), lhsT_scale=w1s[:, t * P:(t + 1) * P],
                                 rhs=gtw[:].bitcast(FP8X4), rhs_scale=gts[:], start=True, stop=True)
 
-        S = [sb.tile([P, 2 * G], F32, name="S%d" % b) for b in range(2)]
-        ce = [sb.tile([P, 2, J], F32, name="ce%d" % b) for b in range(2)]
-        sq = [sb.tile([P, 2, J], F32, name="sq%d" % b) for b in range(2)]
+        Sall = sb.tile([P, 4 * G], F32, name="Sall", tag="dsres", align_bytes=64)
+        ce = [sb.tile([P, n, J], F32, name="ce%d" % t0) for t0, n in SLOTS]
+        sq = [sb.tile([P, n, J], F32, name="sq%d" % t0) for t0, n in SLOTS]
+        cet = [ce[b][:, i, :] for b, (t0, n) in enumerate(SLOTS) for i in range(n)]
         c1 = sb.tile([P, 4, J], F32, name="c1")
         dp = sb.tile([P, 4, J], F32, name="dp")
         dd = sb.tile([P, 4, J], F32, name="dd")
         yy = sb.tile([P, 4, J], F32, name="yy")
         qq = sb.tile([P, 4, J], F32, name="qq")
         uu = sb.tile([P, 4, J], F32, name="uu")
-        for b in range(2):
-            nc.vector.tensor_reduce(S[b][:], A[b][:].rearrange("p t (g i) -> p (t g) i", i=GS), AXX, ALU.add)
-        for b in range(2):
-            nc.vector.scalar_tensor_tensor(ce[b][:].rearrange("p t (g i) -> p (t g) i", i=GS),
-                                           S[b][:].unsqueeze(2).to_broadcast([P, 2 * G, GS]), -1.0 / GS,
-                                           A[b][:].rearrange("p t (g i) -> p (t g) i", i=GS), ALU.mult, ALU.add)
+
+        def grp(ap):
+            return ap.rearrange("p t (g i) -> p (t g) i", i=GS)
+
+        def sums(b):
+            t0, n = SLOTS[b]
+            nc.vector.tensor_reduce(Sall[:, t0 * G:(t0 + n) * G], grp(A[b][:]), AXX, ALU.add)
+
+        def centre(b):
+            t0, n = SLOTS[b]
+            nc.vector.scalar_tensor_tensor(grp(ce[b][:]), Sall[:, t0 * G:(t0 + n) * G].unsqueeze(2).to_broadcast([P, n * G, GS]), -1.0 / GS,
+                                           grp(A[b][:]), ALU.mult, ALU.add)
             nc.scalar.activation(sq[b][:], ce[b][:], ACT.Square)
-            for t in (2 * b, 2 * b + 1):
-                nc.gpsimd.tensor_scalar(dp[:, t, :], sq[b][:, t % 2, :], srs[:, t:t + 1], rr[:, t:t + 1], ALU.mult, ALU.add)
-                nc.scalar.activation(dd[:, t, :], sq[t // 2][:, t % 2, :], ACT.Square, bias=1.0, scale=sh[:, t:t + 1])
+            for t in range(t0, t0 + n):
+                if t < 2:
+                    nc.gpsimd.tensor_scalar(dp[:, t, :], sq[b][:, t - t0, :], srs[:, t:t + 1], rr[:, t:t + 1], ALU.mult, ALU.add)
+                else:
+                    nc.scalar.activation(dp[:, t, :], sq[b][:, t - t0, :], ACT.Identity, bias=rr[:, t:t + 1], scale=srs[:, t:t + 1])
+
+        sums(0)
+        sums(1)
+        centre(0)
+        sums(2)
+        centre(1)
+        centre(2)
+        for b, (t0, n) in enumerate(SLOTS):
+            for t in range(t0, t0 + n):
+                nc.scalar.activation(dd[:, t, :], sq[b][:, t - t0, :], ACT.Square, bias=1.0, scale=sh[:, t:t + 1])
         nc.vector.tensor_copy(gdw[:], dw[:].indirect(offsets[:]))
         TA = [ps.tile([P, 4, H], F32, name="TA%d" % h) for h in range(2)]
         for h in range(2):
@@ -114,7 +135,11 @@ def tile_attend_tcontrastpool_o_pl_kernel(tc, dtab_words, dtab_scales, tab_words
                 nc.tensor.matmul_mx(TA[h][:, t, :], lhsT=w1c[:, t * P:(t + 1) * P].bitcast(FP8X4), lhsT_scale=w1s[:, t * P:(t + 1) * P],
                                     rhs=gdw[:, h * H:(h + 1) * H].bitcast(FP8X4), rhs_scale=gds[4:P, h * H:(h + 1) * H], start=True, stop=True)
         for t in range(4):
-            nc.vector.scalar_tensor_tensor(c1[:, t, :], ce[t // 2][:, t % 2, :], s2[:, t:t + 1], A[t // 2][:, t % 2, :], ALU.mult, ALU.mult)
+            nc.vector.scalar_tensor_tensor(c1[:, t, :], cet[t], s2[:, t:t + 1], At[t], ALU.mult, ALU.mult)
+            if t == 1:
+                nc.vector.tensor_tensor(uu[:, 0:2, :], dp[:, 0:2, :], c1[:, 0:2, :], ALU.add)
+            if t >= 2:
+                nc.gpsimd.tensor_tensor(uu[:, t, :], dp[:, t, :], c1[:, t, :], ALU.add)
         worg = sb.tile([P, 4, P, 4], BF16, name="worg", align_bytes=64)
         woro = worg[:].rearrange("p t m j -> p m j t")
         wori = wor_r[:].rearrange("p j (m t) -> p m j t", t=4)
@@ -138,7 +163,6 @@ def tile_attend_tcontrastpool_o_pl_kernel(tc, dtab_words, dtab_scales, tab_words
         yb = [sb.tile([P, w, 4], BF16, name="yb%d" % n, align_bytes=64) for n, (j0, w) in enumerate(PIECES)]
         for h in range(2):
             nc.vector.tensor_reduce(TS[h][:].rearrange("p t g -> p (t g)"), TA[h][:].rearrange("p t (g i) -> p (t g) i", i=GS), AXX, ALU.add)
-        nc.vector.tensor_tensor(uu[:], dp[:], c1[:], ALU.add)
         worc = sb.tile([P, F], U32, name="worc", align_bytes=64)
         wors = sb.tile([P, F], U8, name="wors", align_bytes=64)
         yc = sb.tile([P, J], U32, name="yc", align_bytes=64)
@@ -152,12 +176,16 @@ def tile_attend_tcontrastpool_o_pl_kernel(tc, dtab_words, dtab_scales, tab_words
         def ilo(ap):
             return ap.rearrange("p (c i) t -> p c t i", i=4)
 
-        def products(n):
+        def prod2(n):
             j0, w = PIECES[n]
             h, b0 = divmod(j0, H)
-            nc.vector.tensor_tensor(x2[n][:].rearrange("p t (g i) -> p t g i", i=GS),
+            (nc.gpsimd if n == 0 else nc.vector).tensor_tensor(x2[n][:].rearrange("p t (g i) -> p t g i", i=GS),
                                     c1[:, :, j0:j0 + w].rearrange("p t (g i) -> p t g i", i=GS),
                                     TS[h][:, :, b0 // GS:(b0 + w) // GS].unsqueeze(3).to_broadcast([P, 4, w // GS, GS]), ALU.mult)
+
+        def prod1(n):
+            j0, w = PIECES[n]
+            h, b0 = divmod(j0, H)
             nc.vector.tensor_tensor(x1[n][:], TA[h][:, :, b0:b0 + w], uu[:, :, j0:j0 + w], ALU.mult)
 
         def combine(n):
@@ -187,27 +215,29 @@ def tile_attend_tcontrastpool_o_pl_kernel(tc, dtab_words, dtab_scales, tab_words
             j0, w = PIECES[n]
             nc.vector.quantize_mx(yc[:, j0:j0 + w].bitcast(FP8X4), ys[:, j0:j0 + w], yb[n][:].rearrange("p j t -> p (j t)"))
 
-        products(0)
-        products(1)
+        prod2(0)
+        prod1(0)
+        prod1(1)
+        prod1(2)
+        prod2(1)
+        prod2(2)
         combine(0)
-        combine(1)
-        scale(0)
         nc.vector.quantize_mx(worc[:].bitcast(FP8X4), wors[:], worg[:].rearrange("p t m j -> p (t m j)"))
+        scale(0)
         layer2(0)
-        scale(1)
-        products(2)
-        layer2(1)
+        combine(1)
         combine(2)
-        residual(0)
+        scale(1)
+        layer2(1)
         scale(2)
-        residual(1)
         layer2(2)
+        residual(0)
+        residual(1)
+        residual(2)
         planes(0)
         planes(1)
-        nc.scalar.dma_start(o1[:, 0:192], yc[:, 0:192].bitcast(I32))
-        residual(2)
         planes(2)
-        nc.sync.dma_start(o1[:, 192:J], yc[:, 192:J].bitcast(I32))
+        nc.sync.dma_start(o1, yc[:].bitcast(I32))
         for q in range(4):
             eng = nc.sync if q == 3 else nc.scalar
             eng.dma_start(out_2[0, 4 * q:4 * q + 4, :].bitcast(I32), ys[32 * q:32 * q + 4, :].bitcast(I32))

from contextlib import ExitStack

import concourse.mybir as mybir

F32 = mybir.dt.float32
BF16 = mybir.dt.bfloat16
I32 = mybir.dt.int32
U32 = mybir.dt.uint32
U16 = mybir.dt.uint16
U8 = mybir.dt.uint8
FP8X4 = mybir.dt.float8_e4m3fn_x4
ALU = mybir.AluOpType
ACT = mybir.ActivationFunctionType
AXX = mybir.AxisListType.X

P = 128
K, R, F, T, J, G = 512, 512, 512, 2048, 256, 16
GS = J // G
H = J // 2
FLOPS = 2 * (2 * K * R * J + R * F * J)
M_SPLIT = 80
SLOTS = ((0, 1), (1, 1), (2, 2))
PIECES = ((0, 128), (128, 64), (192, 64))


def tile_attend_tcontrastpool_o_pl_kernel(tc, dtab_words, dtab_scales, tab_words, tab_scales, w1, sharp, rs, wor, res, offs,
                                           out_0, out_1, out_2):
    nc = tc.nc
    with ExitStack() as ctx:
        held = ctx.enter_context(tc.tile_pool(name="held", bufs=1))
        sb = ctx.enter_context(tc.tile_pool(name="sb", bufs=1))
        ps = ctx.enter_context(tc.psum_pool(name="ps", bufs=1))

        offsets = held.tile([P, J // 16], U16, name="offsets")
        nc.sync.dma_start(offsets[:], offs)

        ts = sb.tile([P, T], U8, name="ts", align_bytes=64)
        nc.vector.memset(ts[:].bitcast(I32), 0)
        warm = sb.tile([P, 1], F32, name="warm")
        warm2 = sb.tile([P, 1], F32, name="warm2")
        nc.vector.memset(warm[:], 1.0)
        nc.scalar.activation(warm2[:], warm[:], ACT.Abs_reciprocal_sqrt)

        w1r = sb.tile([P, 4, R], F32, name="w1r")
        nc.sync.dma_start(w1r[:], w1.rearrange("(p j) c -> p j c", j=4))
        for q in range(4):
            nc.sync.dma_start(ts[q:P:32, :].bitcast(I32), tab_scales[0, q:16:4, :].bitcast(I32))
        tw = sb.tile([P, T], U32, name="tw", align_bytes=64)
        nc.sync.dma_start(tw[:].bitcast(I32), tab_words[0].rearrange("p n t -> p (n t)").bitcast(I32))
        ds = sb.tile([P, T], U8, name="ds", tag="dsres", align_bytes=64)
        nc.vector.memset(ds[:].bitcast(I32), 0)
        for q in range(4):
            nc.sync.dma_start(ds[4 + q:P:32, :].bitcast(I32), dtab_scales[0, q:16:4, :].bitcast(I32))
        dw = sb.tile([P, T], U32, name="dw", align_bytes=64)
        nc.sync.dma_start(dw[:].bitcast(I32), dtab_words[0].rearrange("p n t -> p (n t)").bitcast(I32))
        wor_r = sb.tile([P, 4, F], F32, name="wor_r")
        nc.sync.dma_start(wor_r[:], wor.rearrange("(p j) c -> p j c", j=4))
        rest = sb.tile([P, 4, J], F32, name="rest")
        nc.sync.dma_start(rest[:], res.rearrange("(p t) j -> p t j", t=4))
        sh = sb.tile([P, 4], F32, name="sh")
        rr = sb.tile([P, 4], F32, name="rr")
        nc.gpsimd.dma_start(sh[:], sharp.rearrange("(p t) o -> p (t o)", t=4))
        nc.gpsimd.dma_start(rr[:], rs.rearrange("(p t) o -> p (t o)", t=4))

        gts = sb.tile([P, J], U8, name="gts", align_bytes=64)
        gtw = sb.tile([P, J], U32, name="gtw", align_bytes=64)
        gdw = sb.tile([P, J], U32, name="gdw", align_bytes=64)
        nc.vector.tensor_copy(gts[:], ts[:].indirect(offsets[:]))

        w1g = sb.tile([P, 4, P, 4], BF16, name="w1g", align_bytes=64)
        w1o = w1g[:].rearrange("p t m j -> p m j t")
        w1i = w1r[:].rearrange("p j (m t) -> p m j t", t=4)
        nc.vector.tensor_copy(w1o[:, :M_SPLIT], w1i[:, :M_SPLIT])
        nc.scalar.copy(w1o[:, M_SPLIT:], w1i[:, M_SPLIT:])
        w1c = sb.tile([P, R], U32, name="w1c", align_bytes=64)
        w1s = sb.tile([P, R], U8, name="w1s", align_bytes=64)
        nc.vector.quantize_mx(w1c[:].bitcast(FP8X4), w1s[:], w1g[:].rearrange("p t m j -> p (t m j)"))
        nc.vector.tensor_copy(gtw[:], tw[:].indirect(offsets[:]))
        gds = sb.tile([P, J], U8, name="gds", align_bytes=64)
        nc.vector.tensor_copy(gds[:], ds[:].indirect(offsets[:]))

        srs = sb.tile([P, 4], F32, name="srs")
        s2 = sb.tile([P, 4], F32, name="s2")
        nc.gpsimd.tensor_tensor(srs[:], sh[:], rr[:], ALU.mult)
        nc.gpsimd.tensor_scalar(s2[:], srs[:], -2.0, 0.0, ALU.mult, ALU.add)

        A = [ps.tile([P, n, J], F32, name="A%d" % t0) for t0, n in SLOTS]
        At = [A[b][:, i, :] for b, (t0, n) in enumerate(SLOTS) for i in range(n)]
        for t in range(4):
            nc.tensor.matmul_mx(At[t], lhsT=w1c[:, t * P:(t + 1) * P].bitcast(FP8X4), lhsT_scale=w1s[:, t * P:(t + 1) * P],
                                rhs=gtw[:].bitcast(FP8X4), rhs_scale=gts[:], start=True, stop=True)

        Sall = sb.tile([P, 4 * G], F32, name="Sall", tag="dsres", align_bytes=64)
        ce = [sb.tile([P, n, J], F32, name="ce%d" % t0) for t0, n in SLOTS]
        sq = [sb.tile([P, n, J], F32, name="sq%d" % t0) for t0, n in SLOTS]
        cet = [ce[b][:, i, :] for b, (t0, n) in enumerate(SLOTS) for i in range(n)]
        c1 = sb.tile([P, 4, J], F32, name="c1")
        dp = sb.tile([P, 4, J], F32, name="dp")
        dd = sb.tile([P, 4, J], F32, name="dd")
        yy = sb.tile([P, 4, J], F32, name="yy")
        qq = sb.tile([P, 4, J], F32, name="qq")
        uu = sb.tile([P, 4, J], F32, name="uu")

        def grp(ap):
            return ap.rearrange("p t (g i) -> p (t g) i", i=GS)

        def sums(b):
            t0, n = SLOTS[b]
            nc.vector.tensor_reduce(Sall[:, t0 * G:(t0 + n) * G], grp(A[b][:]), AXX, ALU.add)

        def centre(b):
            t0, n = SLOTS[b]
            nc.vector.scalar_tensor_tensor(grp(ce[b][:]), Sall[:, t0 * G:(t0 + n) * G].unsqueeze(2).to_broadcast([P, n * G, GS]), -1.0 / GS,
                                           grp(A[b][:]), ALU.mult, ALU.add)
            nc.scalar.activation(sq[b][:], ce[b][:], ACT.Square)
            for t in range(t0, t0 + n):
                if t < 2:
                    nc.gpsimd.tensor_scalar(dp[:, t, :], sq[b][:, t - t0, :], srs[:, t:t + 1], rr[:, t:t + 1], ALU.mult, ALU.add)
                else:
                    nc.scalar.activation(dp[:, t, :], sq[b][:, t - t0, :], ACT.Identity, bias=rr[:, t:t + 1], scale=srs[:, t:t + 1])

        sums(0)
        sums(1)
        centre(0)
        sums(2)
        centre(1)
        centre(2)
        for b, (t0, n) in enumerate(SLOTS):
            for t in range(t0, t0 + n):
                nc.scalar.activation(dd[:, t, :], sq[b][:, t - t0, :], ACT.Square, bias=1.0, scale=sh[:, t:t + 1])
        nc.vector.tensor_copy(gdw[:], dw[:].indirect(offsets[:]))
        TA = [ps.tile([P, 4, H], F32, name="TA%d" % h) for h in range(2)]
        for h in range(2):
            for t in range(4):
                nc.tensor.matmul_mx(TA[h][:, t, :], lhsT=w1c[:, t * P:(t + 1) * P].bitcast(FP8X4), lhsT_scale=w1s[:, t * P:(t + 1) * P],
                                    rhs=gdw[:, h * H:(h + 1) * H].bitcast(FP8X4), rhs_scale=gds[4:P, h * H:(h + 1) * H], start=True, stop=True)
        for t in range(4):
            nc.vector.scalar_tensor_tensor(c1[:, t, :], cet[t], s2[:, t:t + 1], At[t], ALU.mult, ALU.mult)
            if t == 1:
                nc.vector.tensor_tensor(uu[:, 0:2, :], dp[:, 0:2, :], c1[:, 0:2, :], ALU.add)
            if t >= 2:
                nc.gpsimd.tensor_tensor(uu[:, t, :], dp[:, t, :], c1[:, t, :], ALU.add)
        worg = sb.tile([P, 4, P, 4], BF16, name="worg", align_bytes=64)
        woro = worg[:].rearrange("p t m j -> p m j t")
        wori = wor_r[:].rearrange("p j (m t) -> p m j t", t=4)
        for h in range(2):
            js = slice(h * H, (h + 1) * H)
            nc.scalar.activation(yy[:, :, js], dd[:, :, js], ACT.Abs_reciprocal_sqrt)
            nc.scalar.activation(qq[:, :, js], yy[:, :, js], ACT.Square)
            if h == 0:
                nc.scalar.copy(woro, wori)

        TS = [sb.tile([P, 4, G // 2], F32, name="TS%d" % h) for h in range(2)]
        NP = len(PIECES)
        x1 = [sb.tile([P, 4, w], F32, name="x1%d" % n) for n, (j0, w) in enumerate(PIECES)]
        x2 = [sb.tile([P, 4, w], F32, name="x2%d" % n) for n, (j0, w) in enumerate(PIECES)]
        x3 = [sb.tile([P, 4, w], F32, name="x3%d" % n) for n, (j0, w) in enumerate(PIECES)]
        fo = [sb.tile([P, w, 4], BF16, name="fo%d" % n, align_bytes=64) for n, (j0, w) in enumerate(PIECES)]
        foc = [sb.tile([P, w], U32, name="foc%d" % n, align_bytes=64) for n, (j0, w) in enumerate(PIECES)]
        fos = [sb.tile([P, w], U8, name="fos%d" % n, align_bytes=64) for n, (j0, w) in enumerate(PIECES)]
        Y = [ps.tile([P, 4, w], F32, name="Y%d" % n) for n, (j0, w) in enumerate(PIECES)]
        y = [sb.tile([P, 4, w], F32, name="y%d" % n) for n, (j0, w) in enumerate(PIECES)]
        yb = [sb.tile([P, w, 4], BF16, name="yb%d" % n, align_bytes=64) for n, (j0, w) in enumerate(PIECES)]
        for h in range(2):
            nc.vector.tensor_reduce(TS[h][:].rearrange("p t g -> p (t g)"), TA[h][:].rearrange("p t (g i) -> p (t g) i", i=GS), AXX, ALU.add)
        worc = sb.tile([P, F], U32, name="worc", align_bytes=64)
        wors = sb.tile([P, F], U8, name="wors", align_bytes=64)
        yc = sb.tile([P, J], U32, name="yc", align_bytes=64)
        ys = sb.tile([P, J], U8, name="ys", align_bytes=64)
        o0 = out_0.rearrange("(p t) j -> p t j", t=4)
        o1 = out_1[0].rearrange("p n t -> p (n t)").bitcast(I32)

        def il(ap):
            return ap.rearrange("p t (c i) -> p c t i", i=4)

        def ilo(ap):
            return ap.rearrange("p (c i) t -> p c t i", i=4)

        def prod2(n):
            j0, w = PIECES[n]
            h, b0 = divmod(j0, H)
            (nc.gpsimd if n == 0 else nc.vector).tensor_tensor(x2[n][:].rearrange("p t (g i) -> p t g i", i=GS),
                                    c1[:, :, j0:j0 + w].rearrange("p t (g i) -> p t g i", i=GS),
                                    TS[h][:, :, b0 // GS:(b0 + w) // GS].unsqueeze(3).to_broadcast([P, 4, w // GS, GS]), ALU.mult)

        def prod1(n):
            j0, w = PIECES[n]
            h, b0 = divmod(j0, H)
            nc.vector.tensor_tensor(x1[n][:], TA[h][:, :, b0:b0 + w], uu[:, :, j0:j0 + w], ALU.mult)

        def combine(n):
            nc.vector.scalar_tensor_tensor(x3[n][:].rearrange("p t j -> p (t j)"), x2[n][:].rearrange("p t j -> p (t j)"), -1.0 / GS,
                                           x1[n][:].rearrange("p t j -> p (t j)"), ALU.mult, ALU.add)

        def scale(n):
            j0, w = PIECES[n]
            nc.vector.tensor_tensor(ilo(fo[n][:]), il(x3[n][:]), il(qq[:, :, j0:j0 + w]), ALU.mult)

        def layer2(n):
            nc.vector.quantize_mx(foc[n][:].bitcast(FP8X4), fos[n][:], fo[n][:].rearrange("p j t -> p (j t)"))
            for t in range(4):
                nc.tensor.matmul_mx(Y[n][:, t, :], lhsT=worc[:, t * P:(t + 1) * P].bitcast(FP8X4), lhsT_scale=wors[:, t * P:(t + 1) * P],
                                    rhs=foc[n][:].bitcast(FP8X4), rhs_scale=fos[n][:], start=True, stop=True)

        def residual(n):
            j0, w = PIECES[n]
            if n == NP - 1:
                nc.vector.tensor_tensor(ilo(yb[n][:]), il(Y[n][:]), il(rest[:, :, j0:j0 + w]), ALU.add)
            nc.vector.tensor_tensor(y[n][:], Y[n][:], rest[:, :, j0:j0 + w], ALU.add)
            nc.sync.dma_start(o0[:, :, j0:j0 + w], y[n][:])
            if n < NP - 1:
                nc.scalar.copy(ilo(yb[n][:]), il(y[n][:]))

        def planes(n):
            j0, w = PIECES[n]
            nc.vector.quantize_mx(yc[:, j0:j0 + w].bitcast(FP8X4), ys[:, j0:j0 + w], yb[n][:].rearrange("p j t -> p (j t)"))

        prod2(0)
        prod1(0)
        prod1(1)
        prod1(2)
        prod2(1)
        prod2(2)
        combine(0)
        nc.vector.quantize_mx(worc[:].bitcast(FP8X4), wors[:], worg[:].rearrange("p t m j -> p (t m j)"))
        scale(0)
        layer2(0)
        combine(1)
        combine(2)
        scale(1)
        layer2(1)
        scale(2)
        layer2(2)
        residual(0)
        residual(1)
        residual(2)
        planes(0)
        planes(1)
        planes(2)
        nc.sync.dma_start(o1, yc[:].bitcast(I32))
        for q in range(4):
            eng = nc.sync if q == 3 else nc.scalar
            eng.dma_start(out_2[0, 4 * q:4 * q + 4, :].bitcast(I32), ys[32 * q:32 * q + 4, :].bitcast(I32))
